import numpy as np
import ml_dtypes


def mxq(x, axis, fmt="e4m3"):
    dtype, down = {"e4m3": (ml_dtypes.float8_e4m3fn, 7), "e5m2": (ml_dtypes.float8_e5m2, 14)}[fmt]
    v = np.moveaxis(np.asarray(x, np.float32).astype(ml_dtypes.bfloat16).astype(np.float64), axis, -1)
    blocks = v.reshape(v.shape[:-1] + (-1, 32))
    amax = np.abs(blocks).max(-1, keepdims=True)
    byte = np.maximum(np.where(amax > 0, np.frexp(amax)[1] - 1 + 127, 0) - down, 1)
    scale = np.exp2(byte - 127.0)
    codes = (blocks / scale).astype(np.float32).astype(dtype).astype(np.float64)
    return np.moveaxis((codes * scale).reshape(v.shape), -1, axis)


WIDE = False


def mx_kscale(k):
    if not WIDE:
        return np.ones(k)
    levels = np.array([10, -10, 5, -5, 0])
    if k % 512:
        return np.exp2(np.random.permutation(np.resize(levels, k // 32))).repeat(32)
    a = np.empty((k // 512, 16))
    for p in range(k // 512):
        a[p, :8] = np.random.permutation(np.resize(levels, 8))
        for g in range(8):
            far = levels[np.abs(levels - a[p, g]) >= 10]
            a[p, g + 8] = far[np.random.randint(len(far))]
    return np.exp2(a.ravel()).repeat(32)


BF16 = ml_dtypes.bfloat16


def bf(x):
    return np.asarray(x, np.float32).astype(BF16)


def f64(x):
    return np.asarray(x).astype(np.float64)


E2M1 = np.array([0.0, 0.5, 1.0, 1.5, 2.0, 3.0, 4.0, 6.0, -0.0, -0.5, -1.0, -1.5, -2.0, -3.0, -4.0, -6.0])


def pack_weight(w, fmt):
    k, n = w.shape
    w = f64(bf(w)).reshape(k // 32, 32, n)
    amax = np.abs(w).max(1)
    if fmt == "e4m3":
        byte = np.frexp(amax)[1] - 1 + 127 - 7
    else:
        mant, ex = np.frexp(amax / 6.0)
        byte = np.where(mant > 0.5, ex, ex - 1) + 127
    byte = np.clip(np.where(amax > 0, byte, 1), 1, 254)
    scaled = (w * np.exp2(127.0 - byte)[:, None, :]).reshape(k, n).astype(np.float32)
    by_word = np.ascontiguousarray(scaled.reshape(k // 512, 128, 4, n).transpose(0, 1, 3, 2))
    if fmt == "e4m3":
        words = by_word.astype(ml_dtypes.float8_e4m3fn).view(np.uint8)
    else:
        c = by_word.astype(ml_dtypes.float4_e2m1fn).view(np.uint8) & 0xF
        words = c[..., 0::2] | (c[..., 1::2] << 4)
    return np.ascontiguousarray(words), np.ascontiguousarray(byte.astype(np.uint8).reshape(k // 512, 16, n))


def unpack_weight(words, scales, fmt):
    g, p, n, _ = words.shape
    if fmt == "e4m3":
        vals = np.ascontiguousarray(words).view(ml_dtypes.float8_e4m3fn).astype(np.float64)
    else:
        nib = np.empty((g, p, n, 4), np.uint8)
        nib[..., 0::2] = words & 0xF
        nib[..., 1::2] = words >> 4
        vals = E2M1[nib]
    vals = vals * np.repeat(np.exp2(scales.astype(np.float64) - 127.0), 8, axis=1)[..., None]
    return vals.transpose(0, 1, 3, 2).reshape(g * 512, n)
def pack4(w):
    words, scales = pack_weight(w, "e2m1")
    return words.reshape(words.shape[0], 128, -1), scales


def unpack4(words, scales):
    return unpack_weight(words.reshape(words.shape[0], 128, -1, 2), scales, "e2m1")


B, D, K = 1024, 512, 1024


def features(uq, wq, gain):
    return np.tanh(uq @ wq) * gain


def pair_kernel(a, b):
    return (mxq(a, 1, "e4m3") @ mxq(b, 1, "e4m3").T) / np.sqrt(a.shape[-1])


def draw0():
    s, t = mx_kscale(D), mx_kscale(K)
    x = bf(np.random.standard_normal((B, D)) * s)
    xn = bf(np.random.standard_normal((B, D)) * s)
    w_words, w_scales = pack4(np.random.standard_normal((D, K)) / np.sqrt(D) / s[:, None])
    wt_words, wt_scales = pack4(np.random.standard_normal((D, K)) / np.sqrt(D) / s[:, None])
    g1 = bf((1.0 + 0.1 * np.random.standard_normal(K)) * t)
    g2 = bf((1.0 + 0.1 * np.random.standard_normal(K)) / t)
    r = bf(np.random.uniform(0.0, 1.0, B))
    return {"x": x, "xn": xn, "w_words": w_words, "w_scales": w_scales, "wt_words": wt_words, "wt_scales": wt_scales, "g1": g1, "g2": g2, "r": r}


def core(x, xn, w_words, w_scales, wt_words, wt_scales, g1, g2, r):
    xq = mxq(f64(x), 1, "e4m3")
    xnq = mxq(f64(xn), 1, "e4m3")
    wq = unpack4(w_words, w_scales)
    wtq = unpack4(wt_words, wt_scales)
    g1, g2, r = f64(g1), f64(g2), f64(r)
    p = features(xq, wq, g1)
    q = features(xq, wtq, g2)
    pn = features(xnq, wq, g1)
    qn = features(xnq, wtq, g2)
    k0 = pair_kernel(p, q)
    k1 = pair_kernel(pn, qn)
    tgt = 1.0 - np.abs(r[:, None] - r[None, :]) + 0.9 * k1
    return k0 - tgt


def e4m3fn_bytes(y):
    return np.clip(np.asarray(y, np.float64), -448.0, 448.0).astype(np.float32).astype(ml_dtypes.float8_e4m3fn).view(np.uint8)


def e4m3fn_values(b):
    return np.asarray(b, np.uint8).view(ml_dtypes.float8_e4m3fn).astype(np.float64)


def setup_inputs():
    d = draw0()
    x0 = np.asarray(d['xn']).astype(np.float64)
    s = (np.max(np.abs(x0), axis=(0,), keepdims=True) / 448.0).astype(np.float32)
    out = {}
    for k, v in d.items():
        if k == 'xn':
            out['xn_bytes'] = e4m3fn_bytes(x0 / s.astype(np.float64))
            out['xn_scale'] = s
        else:
            out[k] = v
    return out


def reference(x, xn_bytes, xn_scale, w_words, w_scales, wt_words, wt_scales, g1, g2, r):
    return core(x, e4m3fn_values(xn_bytes) * xn_scale.astype(np.float64), w_words, w_scales, wt_words, wt_scales, g1, g2, r)

@@ -1,0 +1,338 @@
+from contextlib import ExitStack
+
+import concourse.mybir as mybir
+from concourse.masks import make_identity
+
+B, D, K = 1024, 512, 1024
+FLOPS = 4 * 2 * B * D * K + 2 * 2 * B * B * K
+
+F32 = mybir.dt.float32
+BF16 = mybir.dt.bfloat16
+I32 = mybir.dt.int32
+U32 = mybir.dt.uint32
+U8 = mybir.dt.uint8
+FP8 = mybir.dt.float8_e4m3fn
+FP8X4 = mybir.dt.float8_e4m3fn_x4
+FP4X4 = mybir.dt.float4_e2m1fn_x4
+ACT = mybir.ActivationFunctionType
+ALU = mybir.AluOpType
+
+P = 128
+PACK = 4
+CHUNK = 256
+NCHUNK = B // CHUNK
+NGROUP = K // (P * PACK)
+NUNIT = 4 * NCHUNK
+HALF = NUNIT // 2
+BANKS_PER_UNIT = 4
+TANH_BUFS = 3
+POOL_BASE = 72
+POOL_PER_READ = 24
+BLOCKS_PER_STEP = 2
+X_LOADS = (1, 1, 2, 4)
+XN_FIRST = 0
+FIRST_BLOCK = 2
+V_TURNS = 4
+LEAD = 2
+COPY_AT = 1
+EARLY = 4
+
+
+def block_order():
+    order = []
+    for c in range(NCHUNK):
+        order.append([(a, c) for a in range(c)])
+        order.append([(c, b) for b in range(c + 1)])
+    return order
+
+
+def tile_kernelbehaviouralmetrictdresidual_w4_kernel(
+    tc, x, xn_bytes, xn_scale, w_words, w_scales, wt_words, wt_scales, g1, g2, r, out
+):
+    nc = tc.nc
+    with ExitStack() as ctx:
+        sb = ctx.enter_context(tc.tile_pool(name="sb", bufs=1))
+        ps = ctx.enter_context(tc.psum_pool(name="ps", bufs=1))
+        ctx.enter_context(tc.manual_schedule())
+
+        def tiles(name, n, shape, dtype):
+            return [sb.tile(shape, dtype, name="%s%d" % (name, i), align_bytes=64) for i in range(n)]
+
+        ident = sb.tile([P, P], F32, name="ident")
+        pick = sb.tile([P, 4], BF16, name="pick")
+        x_loads = [sb.tile([P, n, D], BF16, name="x_load%d" % i, align_bytes=64) for i, n in enumerate(X_LOADS)]
+        xn_rows = tiles("xn_rows", B // P, [P, D], BF16)
+        rows = [t[:, j, :] for t, n in zip(x_loads, X_LOADS) for j in range(n)] + [t[:] for t in xn_rows]
+        xn_raw = tiles("xn_raw", 2, [P, 4, D], U8)
+        xn_scale_col = sb.tile([P, PACK], F32, name="xn_scale_col")
+        xn_scale_all = sb.tile([P, D], F32, name="xn_scale_all")
+        x_turned = tiles("x_turned", 2, [P, 2 * CHUNK], F32)
+        x_codes = tiles("x_codes", 2 * NCHUNK, [P, CHUNK], U32)
+        x_scales = tiles("x_scales", 2 * NCHUNK, [P, CHUNK], U8)
+        words_raw = tiles("words_raw", 2, [P, K // 2], I32)
+        scales_raw = tiles("scales_raw", 2, [P, K // 4], I32)
+        words = tiles("words", 2, [P, 2 * K], U8)
+        scales = tiles("scales", 2, [P, K], U8)
+        gain_raw = sb.tile([2, K], BF16, name="gain_raw")
+        gain_rows = sb.tile([P, K], BF16, name="gain_rows")
+        gain_sb = sb.tile([P, 2, NGROUP * PACK], F32, name="gain_sb")
+        r_all = sb.tile([P, B], BF16, name="r_all")
+        neg_r = sb.tile([P, B // P], F32, name="neg_r")
+        tanh_out = tiles("tanh_out", TANH_BUFS, [P, NGROUP, CHUNK, PACK], F32)
+        feats = sb.tile([P, NGROUP, CHUNK, PACK], BF16, name="feats", align_bytes=64)
+        f_codes = tiles("f_codes", NUNIT, [P, NGROUP * CHUNK], U32)
+        f_scales = tiles("f_scales", NUNIT, [P, NGROUP * CHUNK], U8)
+        acc = tiles("acc", NCHUNK, [P, 2, B], F32)
+
+        proj_banks = [ps.tile([P, 512], F32, name="proj%d" % i) for i in range(BANKS_PER_UNIT)]
+        side_banks = [ps.tile([P, 512], F32, name="side%d" % i) for i in range(3)]
+        gain_ps = ps.tile([P, 2, NGROUP * PACK], F32, name="gain_ps")
+        side_uses = []
+
+        def side_bank(banks):
+            side_uses.append(0)
+            return banks[len(side_uses) % len(banks)]
+
+        def weight_of(u):
+            return (u + 1) % 2
+
+        def chunk_of(u):
+            return u // 2
+
+        def load_x(i):
+            first = sum(X_LOADS[:i]) * P
+            nc.sync.dma_start(out=x_loads[i][:], in_=x[first : first + X_LOADS[i] * P, :].rearrange("(a p) k -> p a k", p=P))
+
+        def load_xn(h):
+            nc.sync.dma_start(out=xn_raw[h][:], in_=xn_bytes[h * 512 : (h + 1) * 512, :].rearrange("(a p) k -> p a k", p=P))
+
+        def load_words(i, src):
+            nc.sync.dma_start(out=words_raw[i][:], in_=src[0].bitcast(I32))
+
+        def load_scales(i, src):
+            for row in range(4):
+                nc.sync.dma_start(out=scales_raw[i][row:P:32, :], in_=src[0][row:16:4, :].bitcast(I32))
+
+        def load_gain(i, src):
+            nc.sync.dma_start(out=gain_raw[i : i + 1, :], in_=src.rearrange("(o k) -> o k", o=1))
+
+        def order_weight(i):
+            for dst, src, run in ((words[i], words_raw[i], 4), (scales[i], scales_raw[i], 2)):
+                nc.vector.tensor_copy(
+                    out=dst[:].bitcast(I32).rearrange("p (g t b w) -> p g t b w", g=NGROUP, t=PACK, w=run),
+                    in_=src[:].rearrange("p (g b t w) -> p g t b w", g=NGROUP, t=PACK, w=run),
+                )
+
+        def spread_xn_scale():
+            bank = side_bank(side_banks)
+            for t in range(PACK):
+                nc.tensor.transpose(bank[:, t * P : (t + 1) * P], xn_scale_col[:, t : t + 1].to_broadcast([P, P]), ident[:])
+            return lambda: nc.vector.tensor_copy(out=xn_scale_all[:].rearrange("p (n t) -> p n t", t=PACK), in_=bank[:].rearrange("p (t n) -> p n t", t=PACK))
+
+        def scale_xn(j):
+            nc.vector.tensor_tensor(out=xn_rows[j][:], in0=xn_raw[j // 4][:, j % 4, :].bitcast(FP8), in1=xn_scale_all[:], op=ALU.mult)
+
+        def turn(c, first, count, copy):
+            bank = side_bank(side_banks)
+            for a in range(count):
+                pairs = rows[2 * c + first + a].bitcast(F32)
+                for u in range(2):
+                    col = (2 * a + u) * P
+                    nc.tensor.transpose(bank[:, col : col + P], pairs[:, u : D // 2 : 2], ident[:])
+            return lambda: copy(
+                out=x_turned[c % 2][:, first * 2 * P : (first + count) * 2 * P].rearrange("p (a n u) -> p a n u", a=count, u=2),
+                in_=bank[:, 0 : count * 2 * P].rearrange("p (a u n) -> p a n u", a=count, u=2),
+            )
+
+        def quantize_x(c, first, count):
+            cols = slice(first * P, (first + count) * P)
+            nc.vector.quantize_mx(
+                out=x_codes[c][:, cols].bitcast(FP8X4),
+                scales=x_scales[c][:, cols],
+                in_=x_turned[c % 2][:, first * 2 * P : (first + count) * 2 * P].bitcast(BF16),
+            )
+
+        def project(u, b):
+            g, a = b % NGROUP, b // NGROUP
+            i, c = weight_of(u), chunk_of(u)
+            for t in range(PACK):
+                slot = g * PACK + t
+                nc.tensor.matmul_mx(
+                    out=proj_banks[b][:, t * P : (t + 1) * P],
+                    lhsT=words[i][:, slot * 2 * P : (slot + 1) * 2 * P].bitcast(FP4X4),
+                    lhsT_scale=scales[i][:, slot * P : (slot + 1) * P],
+                    rhs=x_codes[c][:, a * P : (a + 1) * P].bitcast(FP8X4),
+                    rhs_scale=x_scales[c][:, a * P : (a + 1) * P],
+                    start=True,
+                    stop=True,
+                )
+
+        def tanh(u, b):
+            g, a = b % NGROUP, b // NGROUP
+            nc.scalar.activation(
+                out=tanh_out[u % TANH_BUFS][:, g, a * P : (a + 1) * P, :],
+                in_=proj_banks[b][:].rearrange("p (t n) -> p n t", t=PACK),
+                func=ACT.Tanh,
+            )
+
+        def apply_gain(u, split):
+            i = weight_of(u)
+            for engine, gains, lo, hi in ((nc.gpsimd, gain_sb, 0, split), (nc.vector, gain_ps, split, CHUNK)):
+                engine.tensor_tensor(
+                    out=feats[:, :, lo:hi, :],
+                    in0=tanh_out[u % TANH_BUFS][:, :, lo:hi, :],
+                    in1=gains[:, i, :].rearrange("p (g t) -> p g t", t=PACK).unsqueeze(2).to_broadcast([P, NGROUP, hi - lo, PACK]),
+                    op=ALU.mult,
+                )
+
+        def quantize_feats(u):
+            nc.vector.quantize_mx(
+                out=f_codes[u][:].bitcast(FP8X4), scales=f_scales[u][:], in_=feats[:].rearrange("p g n t -> p (g n t)")
+            )
+
+        def pair_block(nxt, a, b, banks):
+            bank = side_bank(banks)
+            up, uq = nxt * HALF + 2 * a + 1, nxt * HALF + 2 * b
+            for i in range(2):
+                for g in range(NGROUP):
+                    rows = slice(g * CHUNK + i * P, g * CHUNK + (i + 1) * P)
+                    cols = slice(g * CHUNK, (g + 1) * CHUNK)
+                    nc.tensor.matmul_mx(
+                        out=bank[:, i * CHUNK : (i + 1) * CHUNK],
+                        lhsT=f_codes[up][:, rows].bitcast(FP8X4),
+                        lhsT_scale=f_scales[up][:, rows],
+                        rhs=f_codes[uq][:, cols].bitcast(FP8X4),
+                        rhs_scale=f_scales[uq][:, cols],
+                        start=(g == 0),
+                        stop=(g == NGROUP - 1),
+                    )
+            part = acc[a][:, :, b * CHUNK : (b + 1) * CHUNK]
+            nc.vector.scalar_tensor_tensor(
+                out=part,
+                in0=bank[:].rearrange("p (i n) -> p i n", i=2),
+                scalar=-0.9 if nxt else -1.0,
+                in1=part,
+                op0=ALU.mult if nxt else ALU.add,
+                op1=ALU.add,
+            )
+            if nxt:
+                nc.sync.dma_start(
+                    out=out[a * CHUNK : (a + 1) * CHUNK, b * CHUNK : (b + 1) * CHUNK].rearrange("(i p) n -> p i n", p=P),
+                    in_=part,
+                )
+
+        def distance(i):
+            nc.scalar.activation(out=acc[i // 2][:, i % 2, :], in_=r_all[:], func=ACT.Abs, bias=neg_r[:, i : i + 1], scale=1.0)
+
+        def reward_columns():
+            bank = side_bank(side_banks)
+            for i in range(B // P):
+                nc.tensor.matmul(bank[:, 2 * i : 2 * i + 2], lhsT=r_all[:, i * P : (i + 1) * P], rhs=pick[:, 2:4], start=True, stop=True)
+            nc.scalar.copy(out=neg_r[:], in_=bank[:, 0 : 2 * (B // P) : 2])
+
+        def gain_columns():
+            nc.vector.tensor_copy(
+                out=gain_rows[0:2, :].rearrange("p (g t b j) -> p g t b j", g=NGROUP, t=PACK, j=8),
+                in_=gain_raw[:].rearrange("p (g b t j) -> p g t b j", g=NGROUP, t=PACK, j=8),
+            )
+            for slot in range(NGROUP * PACK):
+                nc.tensor.matmul(gain_ps[:, :, slot], lhsT=gain_rows[:, slot * P : (slot + 1) * P], rhs=pick[:, 0:2], start=True, stop=True)
+            return lambda: nc.vector.tensor_copy(out=gain_sb[:], in_=gain_ps[:])
+
+        ready = block_order()
+        last = NUNIT
+        blocks = [[] for s in range(last + 1)]
+        for n, group in enumerate(ready):
+            blocks[HALF + 1 + n].extend([(1, a, b) for a, b in group])
+        blocks[last] = blocks[last - 1][-1:] + blocks[last]
+        blocks[last - 1] = blocks[last - 1][:-1]
+        waiting = [(0, a, b) for group in ready for a, b in group]
+        first_use = {}
+        for s in range(FIRST_BLOCK, last):
+            room = 1 if s < EARLY else BLOCKS_PER_STEP
+            take = waiting[: max(0, room - len(blocks[s]))]
+            waiting = waiting[len(take) :]
+            blocks[s] = take + blocks[s]
+            for nxt, a, b in take:
+                first_use.setdefault(a, s)
+        assert not waiting
+        distance_at = {}
+        for a in range(NCHUNK):
+            distance_at[first_use[a] - 2] = 2 * a
+            distance_at[first_use[a] - 1] = 2 * a + 1
+        turn_at = {2 * c - 3: c for c in range(2, NCHUNK)}
+        for c in range(NCHUNK):
+            turn_at[2 * c + 5] = NCHUNK + c
+
+        for i in (1, 0):
+            nc.vector.memset(scales_raw[i][:], 0)
+        nc.vector.memset(gain_rows[:], 0.0)
+        make_identity(nc, ident[:])
+        nc.scalar.activation(out=pick[:, 0:1], in_=ident[:, 0:1], func=ACT.Copy, scale=1.0 / 32.0)
+        nc.scalar.activation(out=pick[:, 1:2], in_=ident[:, 1:2], func=ACT.Copy)
+        nc.scalar.activation(out=pick[:, 2:4], in_=ident[:, 0:2], func=ACT.Copy, scale=-1.0)
+
+        load_x(0)
+        load_words(1, wt_words)
+        load_scales(1, wt_scales)
+        load_x(1)
+        load_x(2)
+        load_words(0, w_words)
+        load_scales(0, w_scales)
+        load_gain(1, g2)
+        load_gain(0, g1)
+        nc.sync.dma_start(out=xn_scale_col[:], in_=xn_scale.rearrange("o (p t) -> p (o t)", t=PACK))
+        load_xn(0)
+        nc.sync.dma_start(out=r_all[:], in_=r.partition_broadcast(P))
+        load_x(3)
+        load_xn(1)
+
+        turn(0, 0, 1, nc.scalar.copy)()
+        order_weight(1)
+        quantize_x(0, 0, 1)
+        turn(0, 1, 1, nc.vector.tensor_copy)()
+        for b in range(NGROUP):
+            project(0, b)
+        quantize_x(0, 1, 1)
+        for b in range(NGROUP, BANKS_PER_UNIT):
+            project(0, b)
+        copy_second = turn(1, 0, 2, nc.vector.tensor_copy)
+        order_weight(0)
+        copy_gains = gain_columns()
+        copy_second()
+        copy_gains()
+
+        for s in range(-1, last + 1):
+            if s >= 1:
+                quantize_feats(s - 1)
+            todo = blocks[s] if s >= 0 else []
+            if 0 <= s < NUNIT:
+                apply_gain(s, POOL_BASE + POOL_PER_READ * (len(todo) + (1 if turn_at.get(s, NUNIT) < V_TURNS else 0)))
+            if s == 0:
+                quantize_x(1, 0, 2)
+                copy_spread()
+            banks = side_banks if s < last - 1 else side_banks + proj_banks
+            if s in turn_at:
+                copy_turned = turn(turn_at[s], 0, 2, nc.vector.tensor_copy if turn_at[s] < V_TURNS else nc.scalar.copy)
+            for block in todo[:LEAD]:
+                pair_block(*block, banks)
+            for b in range(BANKS_PER_UNIT):
+                if s + 1 < NUNIT:
+                    tanh(s + 1, b)
+                if b == COPY_AT and s in turn_at:
+                    copy_turned()
+                if b > 0 and LEAD + b - 1 < len(todo):
+                    pair_block(*todo[LEAD + b - 1], banks)
+                if s + 2 < NUNIT:
+                    project(s + 2, b)
+                if b == 1 and s == -1:
+                    copy_spread = spread_xn_scale()
+                if b == 3 and s == min(distance_at):
+                    reward_columns()
+                if b == 3 and s in distance_at:
+                    distance(distance_at[s])
+            if XN_FIRST <= s < XN_FIRST + NCHUNK:
+                scale_xn(2 * (s - XN_FIRST))
+                scale_xn(2 * (s - XN_FIRST) + 1)
+            if s in turn_at:
+                quantize_x(turn_at[s], 0, 2)

@@ -27,13 +27,12 @@ HALF = NUNIT // 2
 BANKS_PER_UNIT = 4
 TANH_BUFS = 3
 POOL_BASE = 72
-POOL_PER_READ = 24
+POOL_PER_READ = 20
 BLOCKS_PER_STEP = 2
 X_LOADS = (1, 1, 2, 4)
 XN_FIRST = 0
 FIRST_BLOCK = 2
 V_TURNS = 4
-LEAD = 2
 COPY_AT = 1
 EARLY = 4
 
@@ -59,7 +58,7 @@ def tile_kernelbehaviouralmetrictdresidual_w4_kernel(
             return [sb.tile(shape, dtype, name="%s%d" % (name, i), align_bytes=64) for i in range(n)]
 
         ident = sb.tile([P, P], F32, name="ident")
-        pick = sb.tile([P, 4], BF16, name="pick")
+        pick = sb.tile([P, 6], BF16, name="pick")
         x_loads = [sb.tile([P, n, D], BF16, name="x_load%d" % i, align_bytes=64) for i, n in enumerate(X_LOADS)]
         xn_rows = tiles("xn_rows", B // P, [P, D], BF16)
         rows = [t[:, j, :] for t, n in zip(x_loads, X_LOADS) for j in range(n)] + [t[:] for t in xn_rows]
@@ -76,6 +75,7 @@ def tile_kernelbehaviouralmetrictdresidual_w4_kernel(
         gain_raw = sb.tile([2, K], BF16, name="gain_raw")
         gain_rows = sb.tile([P, K], BF16, name="gain_rows")
         gain_sb = sb.tile([P, 2, NGROUP * PACK], F32, name="gain_sb")
+        r_row = sb.tile([P, B], BF16, name="r_row")
         r_all = sb.tile([P, B], BF16, name="r_all")
         neg_r = sb.tile([P, B // P], F32, name="neg_r")
         tanh_out = tiles("tanh_out", TANH_BUFS, [P, NGROUP, CHUNK, PACK], F32)
@@ -206,6 +206,9 @@ def tile_kernelbehaviouralmetrictdresidual_w4_kernel(
                         start=(g == 0),
                         stop=(g == NGROUP - 1),
                     )
+            return bank
+
+        def finish_block(nxt, a, b, bank):
             part = acc[a][:, :, b * CHUNK : (b + 1) * CHUNK]
             nc.vector.scalar_tensor_tensor(
                 out=part,
@@ -224,11 +227,19 @@ def tile_kernelbehaviouralmetrictdresidual_w4_kernel(
         def distance(i):
             nc.scalar.activation(out=acc[i // 2][:, i % 2, :], in_=r_all[:], func=ACT.Abs, bias=neg_r[:, i : i + 1], scale=1.0)
 
-        def reward_columns():
-            bank = side_bank(side_banks)
+        def spread_rewards():
+            column_bank = side_bank(side_banks)
             for i in range(B // P):
-                nc.tensor.matmul(bank[:, 2 * i : 2 * i + 2], lhsT=r_all[:, i * P : (i + 1) * P], rhs=pick[:, 2:4], start=True, stop=True)
-            nc.scalar.copy(out=neg_r[:], in_=bank[:, 0 : 2 * (B // P) : 2])
+                nc.tensor.matmul(column_bank[:, 2 * i : 2 * i + 2], lhsT=r_row[:, i * P : (i + 1) * P], rhs=pick[:, 2:4], start=True, stop=True)
+            row_bank = side_bank(side_banks)[:].bitcast(BF16)
+            for half in range(2):
+                cols = slice(half * 512, (half + 1) * 512)
+                nc.tensor.matmul(row_bank[:, cols], lhsT=pick[:, 4:5].to_broadcast([P, P]), rhs=r_row[:, cols], start=True, stop=True)
+            return column_bank, row_bank
+
+        def copy_rewards(column_bank, row_bank):
+            nc.scalar.copy(out=r_all[:], in_=row_bank)
+            nc.scalar.copy(out=neg_r[:], in_=column_bank[:, 0 : 2 * (B // P) : 2])
 
         def gain_columns():
             nc.vector.tensor_copy(
@@ -244,8 +255,6 @@ def tile_kernelbehaviouralmetrictdresidual_w4_kernel(
         blocks = [[] for s in range(last + 1)]
         for n, group in enumerate(ready):
             blocks[HALF + 1 + n].extend([(1, a, b) for a, b in group])
-        blocks[last] = blocks[last - 1][-1:] + blocks[last]
-        blocks[last - 1] = blocks[last - 1][:-1]
         waiting = [(0, a, b) for group in ready for a, b in group]
         first_use = {}
         for s in range(FIRST_BLOCK, last):
@@ -267,10 +276,12 @@ def tile_kernelbehaviouralmetrictdresidual_w4_kernel(
         for i in (1, 0):
             nc.vector.memset(scales_raw[i][:], 0)
         nc.vector.memset(gain_rows[:], 0.0)
+        nc.vector.memset(r_row[:], 0.0)
         make_identity(nc, ident[:])
         nc.scalar.activation(out=pick[:, 0:1], in_=ident[:, 0:1], func=ACT.Copy, scale=1.0 / 32.0)
         nc.scalar.activation(out=pick[:, 1:2], in_=ident[:, 1:2], func=ACT.Copy)
         nc.scalar.activation(out=pick[:, 2:4], in_=ident[:, 0:2], func=ACT.Copy, scale=-1.0)
+        nc.scalar.activation(out=pick[:, 4:6], in_=ident[:, 0:2], func=ACT.Copy)
 
         load_x(0)
         load_words(1, wt_words)
@@ -282,8 +293,8 @@ def tile_kernelbehaviouralmetrictdresidual_w4_kernel(
         load_gain(1, g2)
         load_gain(0, g1)
         nc.sync.dma_start(out=xn_scale_col[:], in_=xn_scale.rearrange("o (p t) -> p (o t)", t=PACK))
+        nc.sync.dma_start(out=r_row[0:1, :], in_=r.rearrange("(o n) -> o n", o=1))
         load_xn(0)
-        nc.sync.dma_start(out=r_all[:], in_=r.partition_broadcast(P))
         load_x(3)
         load_xn(1)
 
@@ -302,37 +313,49 @@ def tile_kernelbehaviouralmetrictdresidual_w4_kernel(
         copy_second()
         copy_gains()
 
+        held = None
         for s in range(-1, last + 1):
+            todo = blocks[s] if s >= 0 else []
+            banks = side_banks if s < last - 1 else side_banks + proj_banks
             if s >= 1:
                 quantize_feats(s - 1)
-            todo = blocks[s] if s >= 0 else []
+            reads = (1 if held else 0) + max(0, len(todo) - 1) + (1 if turn_at.get(s, NUNIT) < V_TURNS else 0)
+            if held:
+                finish_block(*held)
+                held = None
+            elif s >= 1:
+                scale_xn(2 * s - 1)
             if 0 <= s < NUNIT:
-                apply_gain(s, POOL_BASE + POOL_PER_READ * (len(todo) + (1 if turn_at.get(s, NUNIT) < V_TURNS else 0)))
+                apply_gain(s, POOL_BASE + POOL_PER_READ * reads)
             if s == 0:
                 quantize_x(1, 0, 2)
                 copy_spread()
-            banks = side_banks if s < last - 1 else side_banks + proj_banks
             if s in turn_at:
                 copy_turned = turn(turn_at[s], 0, 2, nc.vector.tensor_copy if turn_at[s] < V_TURNS else nc.scalar.copy)
-            for block in todo[:LEAD]:
-                pair_block(*block, banks)
             for b in range(BANKS_PER_UNIT):
+                if b < len(todo):
+                    made = todo[b] + (pair_block(*todo[b], banks),)
+                    if b + 1 < len(todo) or s == last:
+                        finish_block(*made)
+                    else:
+                        held = made
                 if s + 1 < NUNIT:
                     tanh(s + 1, b)
                 if b == COPY_AT and s in turn_at:
                     copy_turned()
-                if b > 0 and LEAD + b - 1 < len(todo):
-                    pair_block(*todo[LEAD + b - 1], banks)
                 if s + 2 < NUNIT:
                     project(s + 2, b)
                 if b == 1 and s == -1:
                     copy_spread = spread_xn_scale()
-                if b == 3 and s == min(distance_at):
-                    reward_columns()
+                if b == 3 and s == -1:
+                    rewards = spread_rewards()
+                if b == 2 and s == 0:
+                    copy_rewards(*rewards)
                 if b == 3 and s in distance_at:
                     distance(distance_at[s])
             if XN_FIRST <= s < XN_FIRST + NCHUNK:
                 scale_xn(2 * (s - XN_FIRST))
-                scale_xn(2 * (s - XN_FIRST) + 1)
+                if s > 1:
+                    scale_xn(2 * (s - XN_FIRST) + 1)
             if s in turn_at:
                 quantize_x(turn_at[s], 0, 2)

@@ -19,30 +19,56 @@ ALU = mybir.AluOpType
 
 P = 128
 PACK = 4
-CHUNK = 256
+RUN = 8
+BANK = 512
+CHUNK = 2 * P
+NTILE = B // P
 NCHUNK = B // CHUNK
-NGROUP = K // (P * PACK)
+NPASS = K // (P * PACK)
+NSLOT = NPASS * PACK
 NUNIT = 4 * NCHUNK
 HALF = NUNIT // 2
-BANKS_PER_UNIT = 4
+UNIT_BANKS = 2 * NPASS
+SIDE_BANKS = 3
 TANH_BUFS = 3
-POOL_BASE = 72
-POOL_PER_READ = 20
-BLOCKS_PER_STEP = 2
-X_LOADS = (1, 1, 2, 4)
-XN_FIRST = 0
-FIRST_BLOCK = 2
-V_TURNS = 4
-COPY_AT = 1
-EARLY = 4
+W, WT = 0, 1
+INV_SQRT_K = 1.0 / 32.0
+DISCOUNT = 0.9
+
+X_LOADS = (2, 2, 4)
+POOL_TOKENS = 72
+POOL_TOKENS_PER_BANK = 20
+FULL_PACE = 4
+XN_EARLY = 3
 
 
-def block_order():
-    order = []
+def released_blocks():
+    released = []
     for c in range(NCHUNK):
-        order.append([(a, c) for a in range(c)])
-        order.append([(c, b) for b in range(c + 1)])
-    return order
+        released.append([(a, c) for a in range(c)])
+        released.append([(c, b) for b in range(c + 1)])
+    return released
+
+
+def plan_blocks():
+    released = released_blocks()
+    blocks = [[] for s in range(NUNIT + 1)]
+    for n, group in enumerate(released):
+        blocks[HALF + n + 1].extend([(1, a, b) for a, b in group])
+    waiting = [(0, a, b) for group in released for a, b in group]
+    first_step = 2
+    first_use = {}
+    for s in range(first_step, NUNIT):
+        pace = 1 if s < FULL_PACE else 2
+        take = waiting[: max(0, pace - len(blocks[s]))]
+        waiting = waiting[len(take) :]
+        blocks[s] = take + blocks[s]
+        for half, a, b in take:
+            first_use.setdefault(a, s)
+    assert not waiting
+    distance_at = {first_use[i // 2] - 2 + i % 2: i for i in range(NTILE)}
+    assert len(distance_at) == NTILE
+    return blocks, distance_at
 
 
 def tile_kernelbehaviouralmetrictdresidual_w4_kernel(
@@ -58,11 +84,11 @@ def tile_kernelbehaviouralmetrictdresidual_w4_kernel(
             return [sb.tile(shape, dtype, name="%s%d" % (name, i), align_bytes=64) for i in range(n)]
 
         ident = sb.tile([P, P], F32, name="ident")
-        pick = sb.tile([P, 6], BF16, name="pick")
+        pick = sb.tile([P, 3], BF16, name="pick")
         x_loads = [sb.tile([P, n, D], BF16, name="x_load%d" % i, align_bytes=64) for i, n in enumerate(X_LOADS)]
-        xn_rows = tiles("xn_rows", B // P, [P, D], BF16)
-        rows = [t[:, j, :] for t, n in zip(x_loads, X_LOADS) for j in range(n)] + [t[:] for t in xn_rows]
-        xn_raw = tiles("xn_raw", 2, [P, 4, D], U8)
+        xn_rows = tiles("xn_rows", NTILE, [P, D], BF16)
+        token_rows = [t[:, j, :] for t, n in zip(x_loads, X_LOADS) for j in range(n)] + [t[:] for t in xn_rows]
+        xn_raw = tiles("xn_raw", 2, [P, NTILE // 2, D], U8)
         xn_scale_col = sb.tile([P, PACK], F32, name="xn_scale_col")
         xn_scale_all = sb.tile([P, D], F32, name="xn_scale_all")
         x_turned = tiles("x_turned", 2, [P, 2 * CHUNK], F32)
@@ -74,72 +100,93 @@ def tile_kernelbehaviouralmetrictdresidual_w4_kernel(
         scales = tiles("scales", 2, [P, K], U8)
         gain_raw = sb.tile([2, K], BF16, name="gain_raw")
         gain_rows = sb.tile([P, K], BF16, name="gain_rows")
-        gain_sb = sb.tile([P, 2, NGROUP * PACK], F32, name="gain_sb")
+        gain_sb = sb.tile([P, 2, NSLOT], F32, name="gain_sb")
         r_row = sb.tile([P, B], BF16, name="r_row")
         r_all = sb.tile([P, B], BF16, name="r_all")
-        neg_r = sb.tile([P, B // P], F32, name="neg_r")
-        tanh_out = tiles("tanh_out", TANH_BUFS, [P, NGROUP, CHUNK, PACK], F32)
-        feats = sb.tile([P, NGROUP, CHUNK, PACK], BF16, name="feats", align_bytes=64)
-        f_codes = tiles("f_codes", NUNIT, [P, NGROUP * CHUNK], U32)
-        f_scales = tiles("f_scales", NUNIT, [P, NGROUP * CHUNK], U8)
+        neg_r = sb.tile([P, NTILE], F32, name="neg_r")
+        tanh_out = tiles("tanh_out", TANH_BUFS, [P, NPASS, CHUNK, PACK], F32)
+        feats = sb.tile([P, NPASS, CHUNK, PACK], BF16, name="feats", align_bytes=64)
+        f_codes = tiles("f_codes", NUNIT, [P, NPASS * CHUNK], U32)
+        f_scales = tiles("f_scales", NUNIT, [P, NPASS * CHUNK], U8)
         acc = tiles("acc", NCHUNK, [P, 2, B], F32)
 
-        proj_banks = [ps.tile([P, 512], F32, name="proj%d" % i) for i in range(BANKS_PER_UNIT)]
-        side_banks = [ps.tile([P, 512], F32, name="side%d" % i) for i in range(3)]
-        gain_ps = ps.tile([P, 2, NGROUP * PACK], F32, name="gain_ps")
-        side_uses = []
+        proj_banks = [ps.tile([P, BANK], F32, name="proj%d" % i) for i in range(UNIT_BANKS)]
+        side_banks = [ps.tile([P, BANK], F32, name="side%d" % i) for i in range(SIDE_BANKS)]
+        gain_ps = ps.tile([P, 2, NSLOT], F32, name="gain_ps")
+        handed_out = []
 
-        def side_bank(banks):
-            side_uses.append(0)
-            return banks[len(side_uses) % len(banks)]
-
-        def weight_of(u):
-            return (u + 1) % 2
-
-        def chunk_of(u):
-            return u // 2
+        def next_bank(banks):
+            handed_out.append(banks[(len(handed_out) + 1) % len(banks)])
+            return handed_out[-1]
 
         def load_x(i):
             first = sum(X_LOADS[:i]) * P
             nc.sync.dma_start(out=x_loads[i][:], in_=x[first : first + X_LOADS[i] * P, :].rearrange("(a p) k -> p a k", p=P))
 
-        def load_xn(h):
-            nc.sync.dma_start(out=xn_raw[h][:], in_=xn_bytes[h * 512 : (h + 1) * 512, :].rearrange("(a p) k -> p a k", p=P))
+        def load_xn(i):
+            nc.sync.dma_start(out=xn_raw[i][:], in_=xn_bytes[i * B // 2 : (i + 1) * B // 2, :].rearrange("(a p) k -> p a k", p=P))
 
-        def load_words(i, src):
-            nc.sync.dma_start(out=words_raw[i][:], in_=src[0].bitcast(I32))
+        def load_weight(i, src_words, src_scales):
+            nc.sync.dma_start(out=words_raw[i][:], in_=src_words[0].bitcast(I32))
+            for j in range(4):
+                nc.sync.dma_start(out=scales_raw[i][j:P:32, :], in_=src_scales[0][j:16:4, :].bitcast(I32))
 
-        def load_scales(i, src):
-            for row in range(4):
-                nc.sync.dma_start(out=scales_raw[i][row:P:32, :], in_=src[0][row:16:4, :].bitcast(I32))
-
-        def load_gain(i, src):
-            nc.sync.dma_start(out=gain_raw[i : i + 1, :], in_=src.rearrange("(o k) -> o k", o=1))
+        def load_row(dst, src):
+            nc.sync.dma_start(out=dst, in_=src.rearrange("(o n) -> o n", o=1))
 
         def order_weight(i):
-            for dst, src, run in ((words[i], words_raw[i], 4), (scales[i], scales_raw[i], 2)):
+            for dst, src, run_words in ((words[i], words_raw[i], 4), (scales[i], scales_raw[i], 2)):
                 nc.vector.tensor_copy(
-                    out=dst[:].bitcast(I32).rearrange("p (g t b w) -> p g t b w", g=NGROUP, t=PACK, w=run),
-                    in_=src[:].rearrange("p (g b t w) -> p g t b w", g=NGROUP, t=PACK, w=run),
+                    out=dst[:].bitcast(I32).rearrange("p (g t b w) -> p g t b w", g=NPASS, t=PACK, w=run_words),
+                    in_=src[:].rearrange("p (g b t w) -> p g t b w", g=NPASS, t=PACK, w=run_words),
                 )
 
+        def order_gains():
+            nc.vector.tensor_copy(
+                out=gain_rows[0:2, :].rearrange("p (g t b j) -> p g t b j", g=NPASS, t=PACK, j=RUN),
+                in_=gain_raw[:].rearrange("p (g b t j) -> p g t b j", g=NPASS, t=PACK, j=RUN),
+            )
+
+        def gain_columns():
+            for slot in range(NSLOT):
+                nc.tensor.matmul(gain_ps[:, :, slot], lhsT=gain_rows[:, slot * P : (slot + 1) * P], rhs=pick[:, 0:2], start=True, stop=True)
+            nc.vector.tensor_copy(out=gain_sb[:], in_=gain_ps[:])
+
         def spread_xn_scale():
-            bank = side_bank(side_banks)
+            bank = next_bank(side_banks)
             for t in range(PACK):
                 nc.tensor.transpose(bank[:, t * P : (t + 1) * P], xn_scale_col[:, t : t + 1].to_broadcast([P, P]), ident[:])
-            return lambda: nc.vector.tensor_copy(out=xn_scale_all[:].rearrange("p (n t) -> p n t", t=PACK), in_=bank[:].rearrange("p (t n) -> p n t", t=PACK))
+            nc.scalar.copy(out=xn_scale_all[:].rearrange("p (n t) -> p n t", t=PACK), in_=bank[:].rearrange("p (t n) -> p n t", t=PACK))
+
+        def spread_rewards():
+            column_bank = next_bank(side_banks)
+            for i in range(NTILE):
+                nc.tensor.matmul(column_bank[:, i : i + 1], lhsT=r_row[:, i * P : (i + 1) * P], rhs=pick[:, 2:3], start=True, stop=True)
+            row_bank = next_bank(side_banks)[:].bitcast(BF16)
+            for first in range(0, B, BANK):
+                cols = slice(first, first + BANK)
+                nc.tensor.matmul(row_bank[:, cols], lhsT=pick[:, 1:2].to_broadcast([P, P]), rhs=r_row[:, cols], start=True, stop=True)
+            return column_bank, row_bank
+
+        def copy_rewards(column_bank, row_bank):
+            nc.scalar.copy(out=r_all[:], in_=row_bank)
+            nc.scalar.copy(out=neg_r[:], in_=column_bank[:, 0:NTILE])
 
         def scale_xn(j):
-            nc.vector.tensor_tensor(out=xn_rows[j][:], in0=xn_raw[j // 4][:, j % 4, :].bitcast(FP8), in1=xn_scale_all[:], op=ALU.mult)
+            raw = xn_raw[j // (NTILE // 2)][:, j % (NTILE // 2), :]
+            nc.vector.tensor_tensor(out=xn_rows[j][:], in0=raw.bitcast(FP8), in1=xn_scale_all[:], op=ALU.mult)
 
-        def turn(c, first, count, copy):
-            bank = side_bank(side_banks)
+        def turn(c, first, count):
+            bank = next_bank(side_banks)
             for a in range(count):
-                pairs = rows[2 * c + first + a].bitcast(F32)
+                pairs = token_rows[2 * c + first + a].bitcast(F32)
                 for u in range(2):
                     col = (2 * a + u) * P
                     nc.tensor.transpose(bank[:, col : col + P], pairs[:, u : D // 2 : 2], ident[:])
-            return lambda: copy(
+            return bank
+
+        def copy_turned(copy, bank, c, first, count):
+            copy(
                 out=x_turned[c % 2][:, first * 2 * P : (first + count) * 2 * P].rearrange("p (a n u) -> p a n u", a=count, u=2),
                 in_=bank[:, 0 : count * 2 * P].rearrange("p (a u n) -> p a n u", a=count, u=2),
             )
@@ -152,13 +199,16 @@ def tile_kernelbehaviouralmetrictdresidual_w4_kernel(
                 in_=x_turned[c % 2][:, first * 2 * P : (first + count) * 2 * P].bitcast(BF16),
             )
 
-        def project(u, b):
-            g, a = b % NGROUP, b // NGROUP
-            i, c = weight_of(u), chunk_of(u)
+        def weight_of(unit):
+            return WT if unit % 2 == 0 else W
+
+        def project(unit, bank_no):
+            g, a = bank_no % NPASS, bank_no // NPASS
+            i, c = weight_of(unit), unit // 2
             for t in range(PACK):
                 slot = g * PACK + t
                 nc.tensor.matmul_mx(
-                    out=proj_banks[b][:, t * P : (t + 1) * P],
+                    out=proj_banks[bank_no][:, t * P : (t + 1) * P],
                     lhsT=words[i][:, slot * 2 * P : (slot + 1) * 2 * P].bitcast(FP4X4),
                     lhsT_scale=scales[i][:, slot * P : (slot + 1) * P],
                     rhs=x_codes[c][:, a * P : (a + 1) * P].bitcast(FP8X4),
@@ -167,58 +217,58 @@ def tile_kernelbehaviouralmetrictdresidual_w4_kernel(
                     stop=True,
                 )
 
-        def tanh(u, b):
-            g, a = b % NGROUP, b // NGROUP
+        def tanh(unit, bank_no):
+            g, a = bank_no % NPASS, bank_no // NPASS
             nc.scalar.activation(
-                out=tanh_out[u % TANH_BUFS][:, g, a * P : (a + 1) * P, :],
-                in_=proj_banks[b][:].rearrange("p (t n) -> p n t", t=PACK),
+                out=tanh_out[unit % TANH_BUFS][:, g, a * P : (a + 1) * P, :],
+                in_=proj_banks[bank_no][:].rearrange("p (t n) -> p n t", t=PACK),
                 func=ACT.Tanh,
             )
 
-        def apply_gain(u, split):
-            i = weight_of(u)
+        def apply_gain(unit, split):
             for engine, gains, lo, hi in ((nc.gpsimd, gain_sb, 0, split), (nc.vector, gain_ps, split, CHUNK)):
+                by_pass = gains[:, weight_of(unit), :].rearrange("p (g t) -> p g t", t=PACK)
                 engine.tensor_tensor(
                     out=feats[:, :, lo:hi, :],
-                    in0=tanh_out[u % TANH_BUFS][:, :, lo:hi, :],
-                    in1=gains[:, i, :].rearrange("p (g t) -> p g t", t=PACK).unsqueeze(2).to_broadcast([P, NGROUP, hi - lo, PACK]),
+                    in0=tanh_out[unit % TANH_BUFS][:, :, lo:hi, :],
+                    in1=by_pass.unsqueeze(2).to_broadcast([P, NPASS, hi - lo, PACK]),
                     op=ALU.mult,
                 )
 
-        def quantize_feats(u):
+        def quantize_feats(unit):
             nc.vector.quantize_mx(
-                out=f_codes[u][:].bitcast(FP8X4), scales=f_scales[u][:], in_=feats[:].rearrange("p g n t -> p (g n t)")
+                out=f_codes[unit][:].bitcast(FP8X4), scales=f_scales[unit][:], in_=feats[:].rearrange("p g n t -> p (g n t)")
             )
 
-        def pair_block(nxt, a, b, banks):
-            bank = side_bank(banks)
-            up, uq = nxt * HALF + 2 * a + 1, nxt * HALF + 2 * b
+        def multiply_block(half, a, b, banks):
+            bank = next_bank(banks)
+            unit_p, unit_q = half * HALF + 2 * a + 1, half * HALF + 2 * b
             for i in range(2):
-                for g in range(NGROUP):
-                    rows = slice(g * CHUNK + i * P, g * CHUNK + (i + 1) * P)
-                    cols = slice(g * CHUNK, (g + 1) * CHUNK)
+                for g in range(NPASS):
+                    p_cols = slice(g * CHUNK + i * P, g * CHUNK + (i + 1) * P)
+                    q_cols = slice(g * CHUNK, (g + 1) * CHUNK)
                     nc.tensor.matmul_mx(
                         out=bank[:, i * CHUNK : (i + 1) * CHUNK],
-                        lhsT=f_codes[up][:, rows].bitcast(FP8X4),
-                        lhsT_scale=f_scales[up][:, rows],
-                        rhs=f_codes[uq][:, cols].bitcast(FP8X4),
-                        rhs_scale=f_scales[uq][:, cols],
+                        lhsT=f_codes[unit_p][:, p_cols].bitcast(FP8X4),
+                        lhsT_scale=f_scales[unit_p][:, p_cols],
+                        rhs=f_codes[unit_q][:, q_cols].bitcast(FP8X4),
+                        rhs_scale=f_scales[unit_q][:, q_cols],
                         start=(g == 0),
-                        stop=(g == NGROUP - 1),
+                        stop=(g == NPASS - 1),
                     )
             return bank
 
-        def finish_block(nxt, a, b, bank):
+        def finish_block(half, a, b, bank):
             part = acc[a][:, :, b * CHUNK : (b + 1) * CHUNK]
             nc.vector.scalar_tensor_tensor(
                 out=part,
                 in0=bank[:].rearrange("p (i n) -> p i n", i=2),
-                scalar=-0.9 if nxt else -1.0,
+                scalar=-DISCOUNT if half else -1.0,
                 in1=part,
-                op0=ALU.mult if nxt else ALU.add,
+                op0=ALU.mult if half else ALU.add,
                 op1=ALU.add,
             )
-            if nxt:
+            if half:
                 nc.sync.dma_start(
                     out=out[a * CHUNK : (a + 1) * CHUNK, b * CHUNK : (b + 1) * CHUNK].rearrange("(i p) n -> p i n", p=P),
                     in_=part,
@@ -227,135 +277,93 @@ def tile_kernelbehaviouralmetrictdresidual_w4_kernel(
         def distance(i):
             nc.scalar.activation(out=acc[i // 2][:, i % 2, :], in_=r_all[:], func=ACT.Abs, bias=neg_r[:, i : i + 1], scale=1.0)
 
-        def spread_rewards():
-            column_bank = side_bank(side_banks)
-            for i in range(B // P):
-                nc.tensor.matmul(column_bank[:, 2 * i : 2 * i + 2], lhsT=r_row[:, i * P : (i + 1) * P], rhs=pick[:, 2:4], start=True, stop=True)
-            row_bank = side_bank(side_banks)[:].bitcast(BF16)
-            for half in range(2):
-                cols = slice(half * 512, (half + 1) * 512)
-                nc.tensor.matmul(row_bank[:, cols], lhsT=pick[:, 4:5].to_broadcast([P, P]), rhs=r_row[:, cols], start=True, stop=True)
-            return column_bank, row_bank
-
-        def copy_rewards(column_bank, row_bank):
-            nc.scalar.copy(out=r_all[:], in_=row_bank)
-            nc.scalar.copy(out=neg_r[:], in_=column_bank[:, 0 : 2 * (B // P) : 2])
-
-        def gain_columns():
-            nc.vector.tensor_copy(
-                out=gain_rows[0:2, :].rearrange("p (g t b j) -> p g t b j", g=NGROUP, t=PACK, j=8),
-                in_=gain_raw[:].rearrange("p (g b t j) -> p g t b j", g=NGROUP, t=PACK, j=8),
-            )
-            for slot in range(NGROUP * PACK):
-                nc.tensor.matmul(gain_ps[:, :, slot], lhsT=gain_rows[:, slot * P : (slot + 1) * P], rhs=pick[:, 0:2], start=True, stop=True)
-            return lambda: nc.vector.tensor_copy(out=gain_sb[:], in_=gain_ps[:])
-
-        ready = block_order()
-        last = NUNIT
-        blocks = [[] for s in range(last + 1)]
-        for n, group in enumerate(ready):
-            blocks[HALF + 1 + n].extend([(1, a, b) for a, b in group])
-        waiting = [(0, a, b) for group in ready for a, b in group]
-        first_use = {}
-        for s in range(FIRST_BLOCK, last):
-            room = 1 if s < EARLY else BLOCKS_PER_STEP
-            take = waiting[: max(0, room - len(blocks[s]))]
-            waiting = waiting[len(take) :]
-            blocks[s] = take + blocks[s]
-            for nxt, a, b in take:
-                first_use.setdefault(a, s)
-        assert not waiting
-        distance_at = {}
-        for a in range(NCHUNK):
-            distance_at[first_use[a] - 2] = 2 * a
-            distance_at[first_use[a] - 1] = 2 * a + 1
-        turn_at = {2 * c - 3: c for c in range(2, NCHUNK)}
-        for c in range(NCHUNK):
-            turn_at[2 * c + 5] = NCHUNK + c
-
-        for i in (1, 0):
+        for i in (WT, W):
             nc.vector.memset(scales_raw[i][:], 0)
         nc.vector.memset(gain_rows[:], 0.0)
         nc.vector.memset(r_row[:], 0.0)
         make_identity(nc, ident[:])
-        nc.scalar.activation(out=pick[:, 0:1], in_=ident[:, 0:1], func=ACT.Copy, scale=1.0 / 32.0)
-        nc.scalar.activation(out=pick[:, 1:2], in_=ident[:, 1:2], func=ACT.Copy)
-        nc.scalar.activation(out=pick[:, 2:4], in_=ident[:, 0:2], func=ACT.Copy, scale=-1.0)
-        nc.scalar.activation(out=pick[:, 4:6], in_=ident[:, 0:2], func=ACT.Copy)
+        nc.scalar.activation(out=pick[:, 0:1], in_=ident[:, 1:2], func=ACT.Copy, scale=INV_SQRT_K)
+        nc.scalar.activation(out=pick[:, 1:2], in_=ident[:, 0:1], func=ACT.Copy)
+        nc.scalar.activation(out=pick[:, 2:3], in_=ident[:, 0:1], func=ACT.Copy, scale=-1.0)
 
-        load_x(0)
-        load_words(1, wt_words)
-        load_scales(1, wt_scales)
-        load_x(1)
-        load_x(2)
-        load_words(0, w_words)
-        load_scales(0, w_scales)
-        load_gain(1, g2)
-        load_gain(0, g1)
         nc.sync.dma_start(out=xn_scale_col[:], in_=xn_scale.rearrange("o (p t) -> p (o t)", t=PACK))
-        nc.sync.dma_start(out=r_row[0:1, :], in_=r.rearrange("(o n) -> o n", o=1))
+        load_x(0)
+        load_weight(WT, wt_words, wt_scales)
         load_xn(0)
-        load_x(3)
+        load_weight(W, w_words, w_scales)
+        load_row(gain_raw[0:1, :], g2)
+        load_row(gain_raw[1:2, :], g1)
+        load_x(1)
+        load_row(r_row[0:1, :], r)
+        load_x(2)
         load_xn(1)
 
-        turn(0, 0, 1, nc.scalar.copy)()
-        order_weight(1)
-        quantize_x(0, 0, 1)
-        turn(0, 1, 1, nc.vector.tensor_copy)()
-        for b in range(NGROUP):
-            project(0, b)
-        quantize_x(0, 1, 1)
-        for b in range(NGROUP, BANKS_PER_UNIT):
-            project(0, b)
-        copy_second = turn(1, 0, 2, nc.vector.tensor_copy)
-        order_weight(0)
-        copy_gains = gain_columns()
-        copy_second()
-        copy_gains()
+        spread_xn_scale()
+        for a in range(2):
+            copy_turned(nc.scalar.copy, turn(0, a, 1), 0, a, 1)
+        order_weight(WT)
+        for a in range(2):
+            quantize_x(0, a, 1)
+            for g in range(NPASS):
+                project(0, a * NPASS + g)
+        scale_xn(0)
+        order_weight(W)
+        order_gains()
+        scale_xn(1)
 
+        for bank_no in range(UNIT_BANKS):
+            tanh(0, bank_no)
+            project(1, bank_no)
+            if bank_no == 0:
+                gain_columns()
+                scale_xn(XN_EARLY - 1)
+            if bank_no == 1:
+                copy_turned(nc.vector.tensor_copy, turn(1, 0, 2), 1, 0, 2)
+        rewards = spread_rewards()
+
+        blocks, distance_at = plan_blocks()
+        turn_at = {2 * c - 3: c for c in range(2, 2 * NCHUNK)}
+        xn_waiting = list(range(XN_EARLY, NTILE))
         held = None
-        for s in range(-1, last + 1):
-            todo = blocks[s] if s >= 0 else []
-            banks = side_banks if s < last - 1 else side_banks + proj_banks
+        for s in range(NUNIT + 1):
+            todo = blocks[s]
+            turned = turn_at.get(s)
+            vector_turns = turned is not None and turned < NCHUNK
+            vector_banks = (1 if held else 0) + max(0, len(todo) - 1) + (1 if vector_turns or s == 0 else 0)
             if s >= 1:
                 quantize_feats(s - 1)
-            reads = (1 if held else 0) + max(0, len(todo) - 1) + (1 if turn_at.get(s, NUNIT) < V_TURNS else 0)
-            if held:
-                finish_block(*held)
-                held = None
-            elif s >= 1:
-                scale_xn(2 * s - 1)
-            if 0 <= s < NUNIT:
-                apply_gain(s, POOL_BASE + POOL_PER_READ * reads)
+                if held:
+                    finish_block(*held)
+                    held = None
+                else:
+                    scale_xn(xn_waiting[0])
+                    xn_waiting = xn_waiting[1:]
+            if s < NUNIT:
+                apply_gain(s, POOL_TOKENS + POOL_TOKENS_PER_BANK * vector_banks)
             if s == 0:
                 quantize_x(1, 0, 2)
-                copy_spread()
-            if s in turn_at:
-                copy_turned = turn(turn_at[s], 0, 2, nc.vector.tensor_copy if turn_at[s] < V_TURNS else nc.scalar.copy)
-            for b in range(BANKS_PER_UNIT):
-                if b < len(todo):
-                    made = todo[b] + (pair_block(*todo[b], banks),)
-                    if b + 1 < len(todo) or s == last:
+            if turned is not None:
+                turned_bank = turn(turned, 0, 2)
+            banks = side_banks if s + 1 < NUNIT else side_banks + proj_banks
+            for n in range(UNIT_BANKS):
+                if n < len(todo):
+                    made = todo[n] + (multiply_block(*todo[n], banks),)
+                    if n + 1 < len(todo) or s == NUNIT:
                         finish_block(*made)
                     else:
                         held = made
                 if s + 1 < NUNIT:
-                    tanh(s + 1, b)
-                if b == COPY_AT and s in turn_at:
-                    copy_turned()
+                    tanh(s + 1, n)
+                if n == 1 and turned is not None:
+                    copy_turned(nc.vector.tensor_copy if vector_turns else nc.scalar.copy, turned_bank, turned, 0, 2)
                 if s + 2 < NUNIT:
-                    project(s + 2, b)
-                if b == 1 and s == -1:
-                    copy_spread = spread_xn_scale()
-                if b == 3 and s == -1:
-                    rewards = spread_rewards()
-                if b == 2 and s == 0:
-                    copy_rewards(*rewards)
-                if b == 3 and s in distance_at:
-                    distance(distance_at[s])
-            if XN_FIRST <= s < XN_FIRST + NCHUNK:
-                scale_xn(2 * (s - XN_FIRST))
-                if s > 1:
-                    scale_xn(2 * (s - XN_FIRST) + 1)
-            if s in turn_at:
-                quantize_x(turn_at[s], 0, 2)
+                    project(s + 2, n)
+            if s == 0:
+                copy_rewards(*rewards)
+            if s in distance_at:
+                distance(distance_at[s])
+            if xn_waiting:
+                scale_xn(xn_waiting[0])
+                xn_waiting = xn_waiting[1:]
+            if turned is not None:
+                quantize_x(turned, 0, 2)

from contextlib import ExitStack

import concourse.mybir as mybir
from concourse.masks import make_identity

B, D, K = 1024, 512, 1024
FLOPS = 4 * 2 * B * D * K + 2 * 2 * B * B * K

F32 = mybir.dt.float32
BF16 = mybir.dt.bfloat16
I32 = mybir.dt.int32
U32 = mybir.dt.uint32
U8 = mybir.dt.uint8
FP8 = mybir.dt.float8_e4m3fn
FP8X4 = mybir.dt.float8_e4m3fn_x4
FP4X4 = mybir.dt.float4_e2m1fn_x4
ACT = mybir.ActivationFunctionType
ALU = mybir.AluOpType

P = 128
PACK = 4
RUN = 8
BANK = 512
CHUNK = 2 * P
NTILE = B // P
NCHUNK = B // CHUNK
NPASS = K // (P * PACK)
NSLOT = NPASS * PACK
NUNIT = 4 * NCHUNK
HALF = NUNIT // 2
UNIT_BANKS = 2 * NPASS
SIDE_BANKS = 3
TANH_BUFS = 3
W, WT = 0, 1
INV_SQRT_K = 1.0 / 32.0
DISCOUNT = 0.9

X_LOADS = (2, 2, 4)
POOL_TOKENS = 72
POOL_TOKENS_PER_BANK = 20
FULL_PACE = 4
XN_EARLY = 3


def released_blocks():
    released = []
    for c in range(NCHUNK):
        released.append([(a, c) for a in range(c)])
        released.append([(c, b) for b in range(c + 1)])
    return released


def plan_blocks():
    released = released_blocks()
    blocks = [[] for s in range(NUNIT + 1)]
    for n, group in enumerate(released):
        blocks[HALF + n + 1].extend([(1, a, b) for a, b in group])
    waiting = [(0, a, b) for group in released for a, b in group]
    first_step = 2
    first_use = {}
    for s in range(first_step, NUNIT):
        pace = 1 if s < FULL_PACE else 2
        take = waiting[: max(0, pace - len(blocks[s]))]
        waiting = waiting[len(take) :]
        blocks[s] = take + blocks[s]
        for half, a, b in take:
            first_use.setdefault(a, s)
    assert not waiting
    distance_at = {first_use[i // 2] - 2 + i % 2: i for i in range(NTILE)}
    assert len(distance_at) == NTILE
    return blocks, distance_at


def tile_kernelbehaviouralmetrictdresidual_w4_kernel(
    tc, x, xn_bytes, xn_scale, w_words, w_scales, wt_words, wt_scales, g1, g2, r, out
):
    nc = tc.nc
    with ExitStack() as ctx:
        sb = ctx.enter_context(tc.tile_pool(name="sb", bufs=1))
        ps = ctx.enter_context(tc.psum_pool(name="ps", bufs=1))
        ctx.enter_context(tc.manual_schedule())

        def tiles(name, n, shape, dtype):
            return [sb.tile(shape, dtype, name="%s%d" % (name, i), align_bytes=64) for i in range(n)]

        ident = sb.tile([P, P], F32, name="ident")
        pick = sb.tile([P, 3], BF16, name="pick")
        x_loads = [sb.tile([P, n, D], BF16, name="x_load%d" % i, align_bytes=64) for i, n in enumerate(X_LOADS)]
        xn_rows = tiles("xn_rows", NTILE, [P, D], BF16)
        token_rows = [t[:, j, :] for t, n in zip(x_loads, X_LOADS) for j in range(n)] + [t[:] for t in xn_rows]
        xn_raw = tiles("xn_raw", 2, [P, NTILE // 2, D], U8)
        xn_scale_col = sb.tile([P, PACK], F32, name="xn_scale_col")
        xn_scale_all = sb.tile([P, D], F32, name="xn_scale_all")
        x_turned = tiles("x_turned", 2, [P, 2 * CHUNK], F32)
        x_codes = tiles("x_codes", 2 * NCHUNK, [P, CHUNK], U32)
        x_scales = tiles("x_scales", 2 * NCHUNK, [P, CHUNK], U8)
        words_raw = tiles("words_raw", 2, [P, K // 2], I32)
        scales_raw = tiles("scales_raw", 2, [P, K // 4], I32)
        words = tiles("words", 2, [P, 2 * K], U8)
        scales = tiles("scales", 2, [P, K], U8)
        gain_raw = sb.tile([2, K], BF16, name="gain_raw")
        gain_rows = sb.tile([P, K], BF16, name="gain_rows")
        gain_sb = sb.tile([P, 2, NSLOT], F32, name="gain_sb")
        r_row = sb.tile([P, B], BF16, name="r_row")
        r_all = sb.tile([P, B], BF16, name="r_all")
        neg_r = sb.tile([P, NTILE], F32, name="neg_r")
        tanh_out = tiles("tanh_out", TANH_BUFS, [P, NPASS, CHUNK, PACK], F32)
        feats = sb.tile([P, NPASS, CHUNK, PACK], BF16, name="feats", align_bytes=64)
        f_codes = tiles("f_codes", NUNIT, [P, NPASS * CHUNK], U32)
        f_scales = tiles("f_scales", NUNIT, [P, NPASS * CHUNK], U8)
        acc = tiles("acc", NCHUNK, [P, 2, B], F32)

        proj_banks = [ps.tile([P, BANK], F32, name="proj%d" % i) for i in range(UNIT_BANKS)]
        side_banks = [ps.tile([P, BANK], F32, name="side%d" % i) for i in range(SIDE_BANKS)]
        gain_ps = ps.tile([P, 2, NSLOT], F32, name="gain_ps")
        handed_out = []

        def next_bank(banks):
            handed_out.append(banks[(len(handed_out) + 1) % len(banks)])
            return handed_out[-1]

        def load_x(i):
            first = sum(X_LOADS[:i]) * P
            nc.sync.dma_start(out=x_loads[i][:], in_=x[first : first + X_LOADS[i] * P, :].rearrange("(a p) k -> p a k", p=P))

        def load_xn(i):
            nc.sync.dma_start(out=xn_raw[i][:], in_=xn_bytes[i * B // 2 : (i + 1) * B // 2, :].rearrange("(a p) k -> p a k", p=P))

        def load_weight(i, src_words, src_scales):
            nc.sync.dma_start(out=words_raw[i][:], in_=src_words[0].bitcast(I32))
            for j in range(4):
                nc.sync.dma_start(out=scales_raw[i][j:P:32, :], in_=src_scales[0][j:16:4, :].bitcast(I32))

        def load_row(dst, src):
            nc.sync.dma_start(out=dst, in_=src.rearrange("(o n) -> o n", o=1))

        def order_weight(i):
            for dst, src, run_words in ((words[i], words_raw[i], 4), (scales[i], scales_raw[i], 2)):
                nc.vector.tensor_copy(
                    out=dst[:].bitcast(I32).rearrange("p (g t b w) -> p g t b w", g=NPASS, t=PACK, w=run_words),
                    in_=src[:].rearrange("p (g b t w) -> p g t b w", g=NPASS, t=PACK, w=run_words),
                )

        def order_gains():
            nc.vector.tensor_copy(
                out=gain_rows[0:2, :].rearrange("p (g t b j) -> p g t b j", g=NPASS, t=PACK, j=RUN),
                in_=gain_raw[:].rearrange("p (g b t j) -> p g t b j", g=NPASS, t=PACK, j=RUN),
            )

        def gain_columns():
            for slot in range(NSLOT):
                nc.tensor.matmul(gain_ps[:, :, slot], lhsT=gain_rows[:, slot * P : (slot + 1) * P], rhs=pick[:, 0:2], start=True, stop=True)
            nc.vector.tensor_copy(out=gain_sb[:], in_=gain_ps[:])

        def spread_xn_scale():
            bank = next_bank(side_banks)
            for t in range(PACK):
                nc.tensor.transpose(bank[:, t * P : (t + 1) * P], xn_scale_col[:, t : t + 1].to_broadcast([P, P]), ident[:])
            nc.scalar.copy(out=xn_scale_all[:].rearrange("p (n t) -> p n t", t=PACK), in_=bank[:].rearrange("p (t n) -> p n t", t=PACK))

        def spread_rewards():
            column_bank = next_bank(side_banks)
            for i in range(NTILE):
                nc.tensor.matmul(column_bank[:, i : i + 1], lhsT=r_row[:, i * P : (i + 1) * P], rhs=pick[:, 2:3], start=True, stop=True)
            row_bank = next_bank(side_banks)[:].bitcast(BF16)
            for first in range(0, B, BANK):
                cols = slice(first, first + BANK)
                nc.tensor.matmul(row_bank[:, cols], lhsT=pick[:, 1:2].to_broadcast([P, P]), rhs=r_row[:, cols], start=True, stop=True)
            return column_bank, row_bank

        def copy_rewards(column_bank, row_bank):
            nc.scalar.copy(out=r_all[:], in_=row_bank)
            nc.scalar.copy(out=neg_r[:], in_=column_bank[:, 0:NTILE])

        def scale_xn(j):
            raw = xn_raw[j // (NTILE // 2)][:, j % (NTILE // 2), :]
            nc.vector.tensor_tensor(out=xn_rows[j][:], in0=raw.bitcast(FP8), in1=xn_scale_all[:], op=ALU.mult)

        def turn(c, first, count):
            bank = next_bank(side_banks)
            for a in range(count):
                pairs = token_rows[2 * c + first + a].bitcast(F32)
                for u in range(2):
                    col = (2 * a + u) * P
                    nc.tensor.transpose(bank[:, col : col + P], pairs[:, u : D // 2 : 2], ident[:])
            return bank

        def copy_turned(copy, bank, c, first, count):
            copy(
                out=x_turned[c % 2][:, first * 2 * P : (first + count) * 2 * P].rearrange("p (a n u) -> p a n u", a=count, u=2),
                in_=bank[:, 0 : count * 2 * P].rearrange("p (a u n) -> p a n u", a=count, u=2),
            )

        def quantize_x(c, first, count):
            cols = slice(first * P, (first + count) * P)
            nc.vector.quantize_mx(
                out=x_codes[c][:, cols].bitcast(FP8X4),
                scales=x_scales[c][:, cols],
                in_=x_turned[c % 2][:, first * 2 * P : (first + count) * 2 * P].bitcast(BF16),
            )

        def weight_of(unit):
            return WT if unit % 2 == 0 else W

        def project(unit, bank_no):
            g, a = bank_no % NPASS, bank_no // NPASS
            i, c = weight_of(unit), unit // 2
            for t in range(PACK):
                slot = g * PACK + t
                nc.tensor.matmul_mx(
                    out=proj_banks[bank_no][:, t * P : (t + 1) * P],
                    lhsT=words[i][:, slot * 2 * P : (slot + 1) * 2 * P].bitcast(FP4X4),
                    lhsT_scale=scales[i][:, slot * P : (slot + 1) * P],
                    rhs=x_codes[c][:, a * P : (a + 1) * P].bitcast(FP8X4),
                    rhs_scale=x_scales[c][:, a * P : (a + 1) * P],
                    start=True,
                    stop=True,
                )

        def tanh(unit, bank_no):
            g, a = bank_no % NPASS, bank_no // NPASS
            nc.scalar.activation(
                out=tanh_out[unit % TANH_BUFS][:, g, a * P : (a + 1) * P, :],
                in_=proj_banks[bank_no][:].rearrange("p (t n) -> p n t", t=PACK),
                func=ACT.Tanh,
            )

        def apply_gain(unit, split):
            for engine, gains, lo, hi in ((nc.gpsimd, gain_sb, 0, split), (nc.vector, gain_ps, split, CHUNK)):
                by_pass = gains[:, weight_of(unit), :].rearrange("p (g t) -> p g t", t=PACK)
                engine.tensor_tensor(
                    out=feats[:, :, lo:hi, :],
                    in0=tanh_out[unit % TANH_BUFS][:, :, lo:hi, :],
                    in1=by_pass.unsqueeze(2).to_broadcast([P, NPASS, hi - lo, PACK]),
                    op=ALU.mult,
                )

        def quantize_feats(unit):
            nc.vector.quantize_mx(
                out=f_codes[unit][:].bitcast(FP8X4), scales=f_scales[unit][:], in_=feats[:].rearrange("p g n t -> p (g n t)")
            )

        def multiply_block(half, a, b, banks):
            bank = next_bank(banks)
            unit_p, unit_q = half * HALF + 2 * a + 1, half * HALF + 2 * b
            for i in range(2):
                for g in range(NPASS):
                    p_cols = slice(g * CHUNK + i * P, g * CHUNK + (i + 1) * P)
                    q_cols = slice(g * CHUNK, (g + 1) * CHUNK)
                    nc.tensor.matmul_mx(
                        out=bank[:, i * CHUNK : (i + 1) * CHUNK],
                        lhsT=f_codes[unit_p][:, p_cols].bitcast(FP8X4),
                        lhsT_scale=f_scales[unit_p][:, p_cols],
                        rhs=f_codes[unit_q][:, q_cols].bitcast(FP8X4),
                        rhs_scale=f_scales[unit_q][:, q_cols],
                        start=(g == 0),
                        stop=(g == NPASS - 1),
                    )
            return bank

        def finish_block(half, a, b, bank):
            part = acc[a][:, :, b * CHUNK : (b + 1) * CHUNK]
            nc.vector.scalar_tensor_tensor(
                out=part,
                in0=bank[:].rearrange("p (i n) -> p i n", i=2),
                scalar=-DISCOUNT if half else -1.0,
                in1=part,
                op0=ALU.mult if half else ALU.add,
                op1=ALU.add,
            )
            if half:
                nc.sync.dma_start(
                    out=out[a * CHUNK : (a + 1) * CHUNK, b * CHUNK : (b + 1) * CHUNK].rearrange("(i p) n -> p i n", p=P),
                    in_=part,
                )

        def distance(i):
            nc.scalar.activation(out=acc[i // 2][:, i % 2, :], in_=r_all[:], func=ACT.Abs, bias=neg_r[:, i : i + 1], scale=1.0)

        for i in (WT, W):
            nc.vector.memset(scales_raw[i][:], 0)
        nc.vector.memset(gain_rows[:], 0.0)
        nc.vector.memset(r_row[:], 0.0)
        make_identity(nc, ident[:])
        nc.scalar.activation(out=pick[:, 0:1], in_=ident[:, 1:2], func=ACT.Copy, scale=INV_SQRT_K)
        nc.scalar.activation(out=pick[:, 1:2], in_=ident[:, 0:1], func=ACT.Copy)
        nc.scalar.activation(out=pick[:, 2:3], in_=ident[:, 0:1], func=ACT.Copy, scale=-1.0)

        nc.sync.dma_start(out=xn_scale_col[:], in_=xn_scale.rearrange("o (p t) -> p (o t)", t=PACK))
        load_x(0)
        load_weight(WT, wt_words, wt_scales)
        load_xn(0)
        load_weight(W, w_words, w_scales)
        load_row(gain_raw[0:1, :], g2)
        load_row(gain_raw[1:2, :], g1)
        load_x(1)
        load_row(r_row[0:1, :], r)
        load_x(2)
        load_xn(1)

        spread_xn_scale()
        for a in range(2):
            copy_turned(nc.scalar.copy, turn(0, a, 1), 0, a, 1)
        order_weight(WT)
        for a in range(2):
            quantize_x(0, a, 1)
            for g in range(NPASS):
                project(0, a * NPASS + g)
        scale_xn(0)
        order_weight(W)
        order_gains()
        scale_xn(1)

        for bank_no in range(UNIT_BANKS):
            tanh(0, bank_no)
            project(1, bank_no)
            if bank_no == 0:
                gain_columns()
                scale_xn(XN_EARLY - 1)
            if bank_no == 1:
                copy_turned(nc.vector.tensor_copy, turn(1, 0, 2), 1, 0, 2)
        rewards = spread_rewards()

        blocks, distance_at = plan_blocks()
        turn_at = {2 * c - 3: c for c in range(2, 2 * NCHUNK)}
        xn_waiting = list(range(XN_EARLY, NTILE))
        held = None
        for s in range(NUNIT + 1):
            todo = blocks[s]
            turned = turn_at.get(s)
            vector_turns = turned is not None and turned < NCHUNK
            vector_banks = (1 if held else 0) + max(0, len(todo) - 1) + (1 if vector_turns or s == 0 else 0)
            if s >= 1:
                quantize_feats(s - 1)
                if held:
                    finish_block(*held)
                    held = None
                else:
                    scale_xn(xn_waiting[0])
                    xn_waiting = xn_waiting[1:]
            if s < NUNIT:
                apply_gain(s, POOL_TOKENS + POOL_TOKENS_PER_BANK * vector_banks)
            if s == 0:
                quantize_x(1, 0, 2)
            if turned is not None:
                turned_bank = turn(turned, 0, 2)
            banks = side_banks if s + 1 < NUNIT else side_banks + proj_banks
            for n in range(UNIT_BANKS):
                if n < len(todo):
                    made = todo[n] + (multiply_block(*todo[n], banks),)
                    if n + 1 < len(todo) or s == NUNIT:
                        finish_block(*made)
                    else:
                        held = made
                if s + 1 < NUNIT:
                    tanh(s + 1, n)
                if n == 1 and turned is not None:
                    copy_turned(nc.vector.tensor_copy if vector_turns else nc.scalar.copy, turned_bank, turned, 0, 2)
                if s + 2 < NUNIT:
                    project(s + 2, n)
            if s == 0:
                copy_rewards(*rewards)
            if s in distance_at:
                distance(distance_at[s])
            if xn_waiting:
                scale_xn(xn_waiting[0])
                xn_waiting = xn_waiting[1:]
            if turned is not None:
                quantize_x(turned, 0, 2)
